import numpy as np
import ml_dtypes


def mxq(x, axis, fmt="e4m3"):
    dtype, down = {"e4m3": (ml_dtypes.float8_e4m3fn, 7), "e5m2": (ml_dtypes.float8_e5m2, 14)}[fmt]
    v = np.moveaxis(np.asarray(x, np.float32).astype(ml_dtypes.bfloat16).astype(np.float64), axis, -1)
    blocks = v.reshape(v.shape[:-1] + (-1, 32))
    amax = np.abs(blocks).max(-1, keepdims=True)
    byte = np.maximum(np.where(amax > 0, np.frexp(amax)[1] - 1 + 127, 0) - down, 1)
    scale = np.exp2(byte - 127.0)
    codes = (blocks / scale).astype(np.float32).astype(dtype).astype(np.float64)
    return np.moveaxis((codes * scale).reshape(v.shape), -1, axis)


WIDE = False


def mx_kscale(k):
    if not WIDE:
        return np.ones(k)
    levels = np.array([10, -10, 5, -5, 0])
    if k % 512:
        return np.exp2(np.random.permutation(np.resize(levels, k // 32))).repeat(32)
    a = np.empty((k // 512, 16))
    for p in range(k // 512):
        a[p, :8] = np.random.permutation(np.resize(levels, 8))
        for g in range(8):
            far = levels[np.abs(levels - a[p, g]) >= 10]
            a[p, g + 8] = far[np.random.randint(len(far))]
    return np.exp2(a.ravel()).repeat(32)


def f64(x):
    return np.asarray(x).astype(np.float64)


def striped(idx):
    return np.tile(np.asarray(idx).reshape(-1, 16).T, (8, 1)).astype(np.uint16)


def unstriped(offs):
    return offs[:16].T.reshape(-1).astype(np.int64)


E2M1 = np.array([0.0, 0.5, 1.0, 1.5, 2.0, 3.0, 4.0, 6.0, -0.0, -0.5, -1.0, -1.5, -2.0, -3.0, -4.0, -6.0])


def pack_weight(w, fmt):
    k, n = w.shape
    w = f64(np.asarray(w, np.float32).astype(ml_dtypes.bfloat16)).reshape(k // 32, 32, n)
    amax = np.abs(w).max(1)
    if fmt == "e4m3":
        byte = np.frexp(amax)[1] - 1 + 127 - 7
    else:
        mant, ex = np.frexp(amax / 6.0)
        byte = np.where(mant > 0.5, ex, ex - 1) + 127
    byte = np.clip(np.where(amax > 0, byte, 1), 1, 254)
    scaled = (w * np.exp2(127.0 - byte)[:, None, :]).reshape(k, n).astype(np.float32)
    by_word = np.ascontiguousarray(scaled.reshape(k // 512, 128, 4, n).transpose(0, 1, 3, 2))
    if fmt == "e4m3":
        words = by_word.astype(ml_dtypes.float8_e4m3fn).view(np.uint8)
    else:
        c = by_word.astype(ml_dtypes.float4_e2m1fn).view(np.uint8) & 0xF
        words = (c[..., 0::2] | (c[..., 1::2] << 4)).reshape(k // 512, 128, 2 * n)
    return np.ascontiguousarray(words), np.ascontiguousarray(byte.astype(np.uint8).reshape(k // 512, 16, n))


def unpack_weight(words, scales, fmt):
    g, _, n = scales.shape
    words = np.ascontiguousarray(words).reshape(g, 128, n, -1)
    if fmt == "e4m3":
        vals = words.view(ml_dtypes.float8_e4m3fn).astype(np.float64)
    else:
        nib = np.empty((g, 128, n, 4), np.uint8)
        nib[..., 0::2] = words & 0xF
        nib[..., 1::2] = words >> 4
        vals = E2M1[nib]
    vals = vals * np.repeat(np.exp2(scales.astype(np.float64) - 127.0), 8, axis=1)[..., None]
    return vals.transpose(0, 1, 3, 2).reshape(g * 512, n)


D, T, I, J, U, Z, E, Y = 512, 2048, 512, 512, 1024, 1024, 512, 1024


def setup_inputs():
    n = np.random.standard_normal
    idx = np.random.permutation(T)[:I]
    idx2 = np.random.permutation(U)[:J]
    idx3 = np.random.permutation(Z)[:J]
    idx4 = np.random.permutation(Y)[:I]
    fd = mx_kscale(D)
    fi = mx_kscale(I)
    ti = np.ones(T)
    ti[idx] = fi
    ti4 = np.ones(Y)
    ti4[idx4] = fi
    keysp = pack_weight(n((D, T)) / fd[:, None], "e4m3")
    return {
        "keys_words": keysp[0],
        "keys_scales": keysp[1],
        "notes": (n((D, U)) * 1.0 / np.sqrt(D) * fd[:, None]).astype(np.float32),
        "users2": (n((D, Z)) * 1.0 / np.sqrt(D) * fd[:, None]).astype(np.float32),
        "rowf": (np.random.uniform(0.02, 0.08, (I, 1)) * fi[:, None]).astype(np.float32),
        "rowf2": (np.random.uniform(0.02, 0.08, (I, 1)) * fi[:, None]).astype(np.float32),
        "vals": (n((E, T)) / ti).astype(np.float32),
        "vals2": (n((E, Y)) / ti4).astype(np.float32),
        "offs": striped(idx),
        "offs2": striped(idx2),
        "offs3": striped(idx3),
        "offs4": striped(idx4),
    }


def reference(keys_words, keys_scales, notes, users2, rowf, rowf2, vals, vals2, offs, offs2, offs3, offs4):
    idx = unstriped(offs)
    idx2 = unstriped(offs2)
    idx3 = unstriped(offs3)
    idx4 = unstriped(offs4)
    keysu = unpack_weight(keys_words, keys_scales, "e4m3")
    keysidxg = keysu[:, idx]
    notesidx2q = mxq(f64(notes)[:, idx2], 0, "e4m3")
    g1 = keysidxg.T @ notesidx2q
    users2idx3q = mxq(f64(users2)[:, idx3], 0, "e4m3")
    g2 = keysidxg.T @ users2idx3q
    g0 = np.maximum(g1, g2)
    gr1 = g0 * f64(rowf)
    gr2 = g0 * f64(rowf2)
    vt1 = f64(vals)[:, idx].T
    vt2 = f64(vals2)[:, idx4].T
    vt1q = mxq(vt1, 0, "e4m3")
    gr1q = mxq(gr1, 0, "e4m3")
    vt2q = mxq(vt2, 0, "e4m3")
    gr2q = mxq(gr2, 0, "e4m3")
    o = vt1q.T @ gr1q + vt2q.T @ gr2q
    return o

@@ -1,0 +1,259 @@
+from contextlib import ExitStack
+
+import concourse.mybir as mybir
+from concourse.masks import make_identity
+
+D, T, I, J, U, Z, E, Y = 512, 2048, 512, 512, 1024, 1024, 512, 1024
+FLOPS = 4 * 2 * 512 * 512 * 512
+
+F32 = mybir.dt.float32
+BF16 = mybir.dt.bfloat16
+I32 = mybir.dt.int32
+U32 = mybir.dt.uint32
+U16 = mybir.dt.uint16
+U8 = mybir.dt.uint8
+FP8X4 = mybir.dt.float8_e4m3fn_x4
+COPY = mybir.ActivationFunctionType.Copy
+MAX = mybir.AluOpType.max
+MULT = mybir.AluOpType.mult
+
+P = 128
+PACK = 4
+CH = 128
+NCH = J // CH
+
+
+def tile_attend_tab_larger_twostores_kernel(
+    tc, keys_words, keys_scales, notes, users2, rowf, rowf2, vals, vals2, offs, offs2, offs3, offs4, out
+):
+    nc = tc.nc
+    with ExitStack() as ctx:
+        lists = ctx.enter_context(tc.tile_pool(name="lists", bufs=1))
+        keep = ctx.enter_context(tc.tile_pool(name="keep", bufs=1))
+        psum = ctx.enter_context(tc.psum_pool(name="psum", bufs=1))
+
+        def held(shape, dtype, name):
+            return keep.tile(shape, dtype, name=name, align_bytes=64)
+
+        def bank(shape, b, name):
+            return psum.tile(shape, F32, name=name, tag="bank%d" % b)
+
+        idx = lists.tile([P, I // 16], U16, name="idx")
+        idx2 = lists.tile([P, J // 16], U16, name="idx2")
+        idx3 = lists.tile([P, J // 16], U16, name="idx3")
+        idx4 = lists.tile([P, I // 16], U16, name="idx4")
+
+        notes_sb = [held([P, U], F32, "notes%d" % t) for t in range(PACK)]
+        users_sb = [held([P, Z], F32, "users%d" % t) for t in range(PACK)]
+        vals_sb = [held([P, T], F32, "vals%d" % b) for b in range(E // P)]
+        vals2_sb = [held([P, Y], F32, "valsb%d" % b) for b in range(E // P)]
+        kw_sb = held([P, T], U32, "kw_sb")
+        ks_sb = held([P, T], U8, "ks_sb")
+        f1 = held([P, PACK], F32, "f1")
+        f2 = held([P, PACK], F32, "f2")
+        ident = held([P, P], F32, "ident")
+
+        nc.gpsimd.memset(ks_sb[:].bitcast(I32), 0)
+        make_identity(nc, ident[:])
+
+        def load_scales(q):
+            nc.sync.dma_start(
+                out=ks_sb[32 * q : 32 * q + 4, :].bitcast(I32), in_=keys_scales[0, 4 * q : 4 * q + 4, :].bitcast(I32)
+            )
+
+        notes_pl = notes.rearrange("(p t) u -> t p u", t=PACK)
+        users_pl = users2.rearrange("(p t) u -> t p u", t=PACK)
+        nc.sync.dma_start(notes_sb[0][:], notes_pl[0])
+        nc.sync.dma_start(idx2[:], offs2)
+        nc.sync.dma_start(notes_sb[1][:], notes_pl[1])
+        nc.sync.dma_start(notes_sb[2][:], notes_pl[2])
+        load_scales(0)
+        nc.sync.dma_start(notes_sb[3][:], notes_pl[3])
+        load_scales(1)
+        nc.sync.dma_start(idx[:], offs)
+        load_scales(2)
+        nc.sync.dma_start(kw_sb[:].bitcast(I32), keys_words[0].rearrange("p n t -> p (n t)").bitcast(I32))
+        load_scales(3)
+        nc.sync.dma_start(idx3[:], offs3)
+        nc.sync.dma_start(users_sb[0][:], users_pl[0])
+        nc.sync.dma_start(users_sb[1][:], users_pl[1])
+        nc.sync.dma_start(out=f1[:], in_=rowf.rearrange("(p r) o -> p (r o)", r=PACK))
+        nc.sync.dma_start(users_sb[2][:], users_pl[2])
+        nc.sync.dma_start(out=f2[:], in_=rowf2.rearrange("(p r) o -> p (r o)", r=PACK))
+        nc.sync.dma_start(users_sb[3][:], users_pl[3])
+        nc.sync.dma_start(idx4[:], offs4)
+        for b in range(E // P):
+            nc.sync.dma_start(vals2_sb[b][:], vals2[b * P : (b + 1) * P, :])
+        for b in range(E // P):
+            nc.sync.dma_start(vals_sb[b][:], vals[b * P : (b + 1) * P, :])
+
+        def gather_v(dst, window, offsets):
+            nc.vector.tensor_copy(dst, window.indirect(offsets))
+
+        def gather_s(dst, window, offsets):
+            nc.scalar.activation(dst, window.indirect(offsets), COPY)
+
+        def gather_both(dst, window, offsets):
+            gather_v(dst[:, 0:256], window, offsets[:, 0:16])
+            gather_s(dst[:, 256:512], window, offsets[:, 16:32])
+
+        def weave(dst, planes, c0, c1):
+            nc.vector.tensor_copy(
+                out=dst[:, c0:c1, :].rearrange("p (c i) t -> p c t i", i=4),
+                in_=planes[:, :, c0:c1].rearrange("p t (c i) -> p c t i", i=4),
+            )
+
+        def quant(codes, scales, src, c0, c1):
+            nc.vector.quantize_mx(
+                out=codes[:, c0:c1].bitcast(FP8X4),
+                scales=scales[:, c0:c1],
+                in_=src[:, c0:c1, :].rearrange("p c t -> p (c t)"),
+            )
+
+        kq = held([P, I], U32, "kq")
+        kqs = held([P, I], U8, "kqs")
+        n_pl = held([P, PACK, J], BF16, "n_pl")
+        n_il = held([P, J, PACK], BF16, "n_il")
+        nq = held([P, J], U32, "nq")
+        nqs = held([P, J], U8, "nqs")
+        u_pl = held([P, PACK, J], BF16, "u_pl")
+        u_il = held([P, J, PACK], BF16, "u_il")
+        uq = held([P, J], U32, "uq")
+        uqs = held([P, J], U8, "uqs")
+
+        gather_s(n_pl[:, 0, :], notes_sb[0][:], idx2[:])
+        gather_v(n_pl[:, 1, :], notes_sb[1][:], idx2[:])
+        gather_s(n_pl[:, 2, :], notes_sb[2][:], idx2[:])
+        gather_both(n_pl[:, 3, :], notes_sb[3][:], idx2)
+        gather_v(kqs[:].rearrange("p (r s) -> p s r", r=PACK), ks_sb[:], idx[:])
+        weave(n_il, n_pl, 0, 256)
+        weave(n_il, n_pl, 256, 512)
+        quant(nq, nqs, n_il, 0, 256)
+        gather_v(kq[:].rearrange("p (r s) -> p s r", r=PACK), kw_sb[:], idx[:])
+        quant(nq, nqs, n_il, 256, 512)
+
+        def scores(dst, codes, scales, c):
+            cols = slice(c * CH, (c + 1) * CH)
+            for r in range(PACK):
+                rows = slice(r * P, (r + 1) * P)
+                nc.tensor.matmul_mx(
+                    out=dst[:, r, :],
+                    lhsT=kq[:, rows].bitcast(FP8X4),
+                    lhsT_scale=kqs[:, rows],
+                    rhs=codes[:, cols].bitcast(FP8X4),
+                    rhs_scale=scales[:, cols],
+                    start=True,
+                    stop=True,
+                )
+
+        g1_sb = held([P, J, PACK], F32, "g1_sb")
+        gather_s(u_pl[:, 0, :], users_sb[0][:], idx3[:])
+        gather_v(u_pl[:, 1, :], users_sb[1][:], idx3[:])
+        for c in range(NCH):
+            g1 = bank([P, PACK, CH], c, "g1")
+            scores(g1, nq, nqs, c)
+            nc.scalar.copy(out=g1_sb[:, c * CH : (c + 1) * CH, :], in_=g1[:].rearrange("p r j -> p j r"))
+            if c == 1:
+                gather_s(u_pl[:, 2, :], users_sb[2][:], idx3[:])
+        gather_both(u_pl[:, 3, :], users_sb[3][:], idx3)
+
+        g0 = held([P, J, PACK], F32, "g0")
+        gr1 = held([P, J, PACK], BF16, "gr1")
+        gr2 = held([P, J, PACK], BF16, "gr2")
+        g1q = held([P, J], U32, "g1q")
+        g1s = held([P, J], U8, "g1s")
+        g2q = held([P, J], U32, "g2q")
+        g2s = held([P, J], U8, "g2s")
+
+        weave(u_il, u_pl, 0, 256)
+        weave(u_il, u_pl, 256, 512)
+        quant(uq, uqs, u_il, 0, 256)
+        quant(uq, uqs, u_il, 256, 512)
+
+        def larger(c):
+            cols = slice(c * CH, (c + 1) * CH)
+            g2 = bank([P, PACK, CH], c, "g2")
+            scores(g2, uq, uqs, c)
+            nc.vector.tensor_tensor(
+                out=g0[:, cols, :], in0=g2[:].rearrange("p r j -> p j r"), in1=g1_sb[:, cols, :], op=MAX
+            )
+
+        def scale_rows(c):
+            cols = slice(c * CH, (c + 1) * CH)
+            for dst, f in ((gr1, f1), (gr2, f2)):
+                nc.vector.tensor_tensor(
+                    out=dst[:, cols, :],
+                    in0=g0[:, cols, :],
+                    in1=f[:].unsqueeze(1).to_broadcast([P, CH, PACK]),
+                    op=MULT,
+                )
+
+        def turn(name, window, offsets, gather, b):
+            picked = held([P, I], BF16, name + "_picked")
+            gather(picked[:], window[:], offsets)
+            words = picked[:].bitcast(F32)
+            xt = bank([P, 2, P], 4 + b % 2, name + "_xt")
+            for u in range(2):
+                nc.tensor.transpose(xt[:, u, :], words[:, u : I // 2 : 2], ident[:])
+            il = held([P, P, PACK], BF16, name + "_il")
+            nc.scalar.copy(
+                out=il[:].rearrange("p e t -> p (e t)").bitcast(F32).rearrange("p (e u) -> p e u", u=2),
+                in_=xt[:].rearrange("p u e -> p e u"),
+            )
+            return il
+
+        def whole_s(dst, window, offsets):
+            gather_s(dst, window, offsets[:])
+
+        def quant_block(name, il):
+            codes = held([P, P], U32, name + "_q")
+            scales = held([P, P], U8, name + "_s")
+            quant(codes, scales, il, 0, P)
+            return codes, scales
+
+        v2_il = []
+        larger(0)
+        larger(1)
+        v2_il.append(turn("v2_0", vals2_sb[0], idx4, whole_s, 0))
+        scale_rows(0)
+        larger(2)
+        v2_il.append(turn("v2_1", vals2_sb[1], idx4, whole_s, 1))
+        scale_rows(1)
+        larger(3)
+        v2_il.append(turn("v2_2", vals2_sb[2], idx4, whole_s, 0))
+        scale_rows(2)
+        quant(g1q, g1s, gr1, 0, 256)
+        quant(g2q, g2s, gr2, 0, 256)
+        v2_il.append(turn("v2_3", vals2_sb[3], idx4, whole_s, 1))
+        scale_rows(3)
+        v2q = [quant_block("v2_%d" % b, v2_il[b]) for b in range(2)]
+        quant(g1q, g1s, gr1, 256, 512)
+        quant(g2q, g2s, gr2, 256, 512)
+        v2q = v2q + [quant_block("v2_%d" % b, v2_il[b]) for b in range(2, 4)]
+
+        res = held([P, E // P, J], F32, "res")
+        for b in range(E // P):
+            last = b == E // P - 1
+            il = turn("v1_%d" % b, vals_sb[b], idx, gather_both if last else whole_s, b)
+            v1q = quant_block("v1_%d" % b, il)
+            pieces = [(0, 256, 6), (256, 512, 7)] if last else [(0, 512, b)]
+            accs = [bank([P, c1 - c0], bk, "acc") for c0, c1, bk in pieces]
+            for first, (vq, vs), gq, gs in ((True, v2q[b], g2q, g2s), (False, v1q, g1q, g1s)):
+                for acc, (c0, c1, bk) in zip(accs, pieces):
+                    nc.tensor.matmul_mx(
+                        out=acc[:],
+                        lhsT=vq[:].bitcast(FP8X4),
+                        lhsT_scale=vs[:],
+                        rhs=gq[:, c0:c1].bitcast(FP8X4),
+                        rhs_scale=gs[:, c0:c1],
+                        start=first,
+                        stop=not first,
+                    )
+            if last:
+                nc.vector.tensor_copy(out=res[:, b, 0:256], in_=accs[0][:])
+                nc.scalar.copy(out=res[:, b, 256:512], in_=accs[1][:])
+                nc.sync.dma_start(out[b * P : (b + 1) * P, 0:256], res[:, b, 0:256])
+                nc.scalar.dma_start(out[b * P : (b + 1) * P, 256:512], res[:, b, 256:512])
+            else:
+                nc.vector.tensor_copy(out=res[:, b, :], in_=accs[0][:])
+                nc.sync.dma_start(out[b * P : (b + 1) * P, :], res[:, b, :])

@@ -30,10 +30,14 @@ def tile_attend_tab_larger_twostores_kernel(
     with ExitStack() as ctx:
         lists = ctx.enter_context(tc.tile_pool(name="lists", bufs=1))
         keep = ctx.enter_context(tc.tile_pool(name="keep", bufs=1))
+        reuse = ctx.enter_context(tc.tile_pool(name="reuse", bufs=1))
         psum = ctx.enter_context(tc.psum_pool(name="psum", bufs=1))
 
         def held(shape, dtype, name):
             return keep.tile(shape, dtype, name=name, align_bytes=64)
+
+        def placed(shape, dtype, name, kib):
+            return reuse.tile(shape, dtype, name=name, align_bytes=64, offset=kib * 1024)
 
         def bank(shape, b, name):
             return psum.tile(shape, F32, name=name, tag="bank%d" % b)
@@ -44,9 +48,11 @@ def tile_attend_tab_larger_twostores_kernel(
         idx4 = lists.tile([P, I // 16], U16, name="idx4")
 
         notes_sb = [held([P, U], F32, "notes%d" % t) for t in range(PACK)]
-        users_sb = [held([P, Z], F32, "users%d" % t) for t in range(PACK)]
-        vals_sb = [held([P, T], F32, "vals%d" % b) for b in range(E // P)]
-        vals2_sb = [held([P, Y], F32, "valsb%d" % b) for b in range(E // P)]
+        users_sb = [held([P, Z], F32, "users%d" % t) for t in range(PACK - 1)] + [placed([P, Z], F32, "users3", 0)]
+        vals_sb = [placed([P, T], F32, "vals%d" % b, 8 + 8 * b) for b in range(E // P)]
+        vals2_sb = [
+            placed([P, Y], F32, "valsb2", 4) if b == 2 else held([P, Y], F32, "valsb%d" % b) for b in range(E // P)
+        ]
         kw_sb = held([P, T], U32, "kw_sb")
         ks_sb = held([P, T], U8, "ks_sb")
         f1 = held([P, PACK], F32, "f1")
@@ -54,6 +60,8 @@ def tile_attend_tab_larger_twostores_kernel(
         ident = held([P, P], F32, "ident")
 
         nc.gpsimd.memset(ks_sb[:].bitcast(I32), 0)
+        nc.gpsimd.dma_start(out=f2[:], in_=rowf2.rearrange("(p r) o -> p (r o)", r=PACK))
+        nc.gpsimd.dma_start(out=f1[:], in_=rowf.rearrange("(p r) o -> p (r o)", r=PACK))
         make_identity(nc, ident[:])
 
         def load_scales(q):
@@ -66,22 +74,20 @@ def tile_attend_tab_larger_twostores_kernel(
         nc.sync.dma_start(notes_sb[0][:], notes_pl[0])
         nc.sync.dma_start(idx2[:], offs2)
         nc.sync.dma_start(notes_sb[1][:], notes_pl[1])
-        nc.sync.dma_start(notes_sb[2][:], notes_pl[2])
         load_scales(0)
-        nc.sync.dma_start(notes_sb[3][:], notes_pl[3])
         load_scales(1)
-        nc.sync.dma_start(idx[:], offs)
+        nc.sync.dma_start(notes_sb[2][:], notes_pl[2])
         load_scales(2)
-        nc.sync.dma_start(kw_sb[:].bitcast(I32), keys_words[0].rearrange("p n t -> p (n t)").bitcast(I32))
         load_scales(3)
+        nc.sync.dma_start(idx[:], offs)
+        nc.sync.dma_start(notes_sb[3][:], notes_pl[3])
+        nc.sync.dma_start(kw_sb[:].bitcast(I32), keys_words[0].rearrange("p n t -> p (n t)").bitcast(I32))
         nc.sync.dma_start(idx3[:], offs3)
         nc.sync.dma_start(users_sb[0][:], users_pl[0])
         nc.sync.dma_start(users_sb[1][:], users_pl[1])
-        nc.sync.dma_start(out=f1[:], in_=rowf.rearrange("(p r) o -> p (r o)", r=PACK))
-        nc.sync.dma_start(users_sb[2][:], users_pl[2])
-        nc.sync.dma_start(out=f2[:], in_=rowf2.rearrange("(p r) o -> p (r o)", r=PACK))
-        nc.sync.dma_start(users_sb[3][:], users_pl[3])
         nc.sync.dma_start(idx4[:], offs4)
+        nc.sync.dma_start(users_sb[2][:], users_pl[2])
+        nc.sync.dma_start(users_sb[3][:], users_pl[3])
         for b in range(E // P):
             nc.sync.dma_start(vals2_sb[b][:], vals2[b * P : (b + 1) * P, :])
         for b in range(E // P):
@@ -97,8 +103,8 @@ def tile_attend_tab_larger_twostores_kernel(
             gather_v(dst[:, 0:256], window, offsets[:, 0:16])
             gather_s(dst[:, 256:512], window, offsets[:, 16:32])
 
-        def weave(dst, planes, c0, c1):
-            nc.vector.tensor_copy(
+        def weave(dst, planes, c0, c1, copy=nc.vector.tensor_copy):
+            copy(
                 out=dst[:, c0:c1, :].rearrange("p (c i) t -> p c t i", i=4),
                 in_=planes[:, :, c0:c1].rearrange("p t (c i) -> p c t i", i=4),
             )
@@ -123,14 +129,14 @@ def tile_attend_tab_larger_twostores_kernel(
 
         gather_s(n_pl[:, 0, :], notes_sb[0][:], idx2[:])
         gather_v(n_pl[:, 1, :], notes_sb[1][:], idx2[:])
+        gather_v(kqs[:].rearrange("p (r s) -> p s r", r=PACK), ks_sb[:], idx[:])
         gather_s(n_pl[:, 2, :], notes_sb[2][:], idx2[:])
         gather_both(n_pl[:, 3, :], notes_sb[3][:], idx2)
-        gather_v(kqs[:].rearrange("p (r s) -> p s r", r=PACK), ks_sb[:], idx[:])
         weave(n_il, n_pl, 0, 256)
-        weave(n_il, n_pl, 256, 512)
+        weave(n_il, n_pl, 256, 512, nc.scalar.copy)
         quant(nq, nqs, n_il, 0, 256)
-        gather_v(kq[:].rearrange("p (r s) -> p s r", r=PACK), kw_sb[:], idx[:])
         quant(nq, nqs, n_il, 256, 512)
+        gather_v(kq[:].rearrange("p (r s) -> p s r", r=PACK), kw_sb[:], idx[:])
 
         def scores(dst, codes, scales, c):
             cols = slice(c * CH, (c + 1) * CH)
@@ -146,16 +152,19 @@ def tile_attend_tab_larger_twostores_kernel(
                     stop=True,
                 )
 
-        g1_sb = held([P, J, PACK], F32, "g1_sb")
+        g1_half = [held([P, 2, CH, PACK], F32, "g1_lo"), placed([P, 2, CH, PACK], F32, "g1_hi", 0)]
+        g1_sb = [g1_half[c // 2][:, c % 2] for c in range(NCH)]
         gather_s(u_pl[:, 0, :], users_sb[0][:], idx3[:])
         gather_v(u_pl[:, 1, :], users_sb[1][:], idx3[:])
+        g1 = [bank([P, PACK, CH], c, "g1") for c in range(NCH)]
         for c in range(NCH):
-            g1 = bank([P, PACK, CH], c, "g1")
-            scores(g1, nq, nqs, c)
-            nc.scalar.copy(out=g1_sb[:, c * CH : (c + 1) * CH, :], in_=g1[:].rearrange("p r j -> p j r"))
-            if c == 1:
-                gather_s(u_pl[:, 2, :], users_sb[2][:], idx3[:])
+            scores(g1[c], nq, nqs, c)
+        for c in range(2):
+            nc.scalar.copy(out=g1_sb[c], in_=g1[c][:].rearrange("p r j -> p j r"))
+        gather_v(u_pl[:, 2, :], users_sb[2][:], idx3[:])
         gather_both(u_pl[:, 3, :], users_sb[3][:], idx3)
+        for c in range(2, NCH):
+            nc.scalar.copy(out=g1_sb[c], in_=g1[c][:].rearrange("p r j -> p j r"))
 
         g0 = held([P, J, PACK], F32, "g0")
         gr1 = held([P, J, PACK], BF16, "gr1")
@@ -175,85 +184,98 @@ def tile_attend_tab_larger_twostores_kernel(
             g2 = bank([P, PACK, CH], c, "g2")
             scores(g2, uq, uqs, c)
             nc.vector.tensor_tensor(
-                out=g0[:, cols, :], in0=g2[:].rearrange("p r j -> p j r"), in1=g1_sb[:, cols, :], op=MAX
+                out=g0[:, cols, :], in0=g2[:].rearrange("p r j -> p j r"), in1=g1_sb[c], op=MAX
             )
 
-        def scale_rows(c):
-            cols = slice(c * CH, (c + 1) * CH)
-            for dst, f in ((gr1, f1), (gr2, f2)):
-                nc.vector.tensor_tensor(
-                    out=dst[:, cols, :],
-                    in0=g0[:, cols, :],
-                    in1=f[:].unsqueeze(1).to_broadcast([P, CH, PACK]),
-                    op=MULT,
-                )
-
-        def turn(name, window, offsets, gather, b):
-            picked = held([P, I], BF16, name + "_picked")
-            gather(picked[:], window[:], offsets)
-            words = picked[:].bitcast(F32)
-            xt = bank([P, 2, P], 4 + b % 2, name + "_xt")
-            for u in range(2):
-                nc.tensor.transpose(xt[:, u, :], words[:, u : I // 2 : 2], ident[:])
-            il = held([P, P, PACK], BF16, name + "_il")
-            nc.scalar.copy(
-                out=il[:].rearrange("p e t -> p (e t)").bitcast(F32).rearrange("p (e u) -> p e u", u=2),
-                in_=xt[:].rearrange("p u e -> p e u"),
+        def scale_rows(dst, f, h):
+            cols = slice(h * 256, (h + 1) * 256)
+            nc.vector.tensor_tensor(
+                out=dst[:, cols, :],
+                in0=g0[:, cols, :],
+                in1=f[:].unsqueeze(1).to_broadcast([P, 256, PACK]),
+                op=MULT,
             )
-            return il
 
-        def whole_s(dst, window, offsets):
-            gather_s(dst, window, offsets[:])
+        def turn(picked, nblk, bk, il, copy, name):
+            xt = bank([P, nblk, 2, P], bk, name)
+            for n in range(nblk):
+                words = picked[n][:].bitcast(F32)
+                for u in range(2):
+                    nc.tensor.transpose(xt[:, n, u, :], words[:, u : I // 2 : 2], ident[:])
+            copy(
+                out=il.rearrange("p e t -> p (e t)").bitcast(F32).rearrange("p (n e u) -> p n e u", n=nblk, u=2),
+                in_=xt[:].rearrange("p n u e -> p n e u"),
+            )
 
-        def quant_block(name, il):
-            codes = held([P, P], U32, name + "_q")
-            scales = held([P, P], U8, name + "_s")
-            quant(codes, scales, il, 0, P)
-            return codes, scales
+        w_pick = [held([P, I], BF16, "w_pick%d" % b) for b in range(4)]
+        v_pick = [held([P, I], BF16, "v_pick%d" % b) for b in range(4)]
+        w_il = [placed([P, 256, PACK], BF16, "w_il01", 4), placed([P, 256, PACK], BF16, "w_il23", 8)]
+        v_il0 = placed([P, P, PACK], BF16, "v_il0", 16)
+        v_il1 = placed([P, P, PACK], BF16, "v_il1", 24)
+        v_il23 = placed([P, 256, PACK], BF16, "v_il23", 36)
+        wq = held([P, E], U32, "wq")
+        ws = held([P, E], U8, "ws")
+        vq = [placed([P, 256], U32, "vq01", 38), held([P, 256], U32, "vq23")]
+        vs = held([P, E], U8, "vs")
+        res = [placed([P, J], F32, "res0", 32), placed([P, J], F32, "res1", 34), held([P, J], F32, "res2"), held([P, J], F32, "res3")]
 
-        v2_il = []
+        def quant_into(codes, scales, src):
+            nc.vector.quantize_mx(out=codes.bitcast(FP8X4), scales=scales, in_=src.rearrange("p c t -> p (c t)"))
+
+        def product(acc, lq, ls, gq, gs, first):
+            nc.tensor.matmul_mx(
+                out=acc[:],
+                lhsT=lq.bitcast(FP8X4),
+                lhsT_scale=ls,
+                rhs=gq[:].bitcast(FP8X4),
+                rhs_scale=gs[:],
+                start=first,
+                stop=not first,
+            )
+
+        def blk(b):
+            return slice(b * P, (b + 1) * P)
+
+        gather_s(w_pick[0][:], vals2_sb[0][:], idx4[:])
         larger(0)
         larger(1)
-        v2_il.append(turn("v2_0", vals2_sb[0], idx4, whole_s, 0))
-        scale_rows(0)
+        gather_s(w_pick[1][:], vals2_sb[1][:], idx4[:])
         larger(2)
-        v2_il.append(turn("v2_1", vals2_sb[1], idx4, whole_s, 1))
-        scale_rows(1)
+        scale_rows(gr2, f2, 0)
         larger(3)
-        v2_il.append(turn("v2_2", vals2_sb[2], idx4, whole_s, 0))
-        scale_rows(2)
-        quant(g1q, g1s, gr1, 0, 256)
+        gather_s(w_pick[2][:], vals2_sb[2][:], idx4[:])
+        turn(w_pick[0:2], 2, 4, w_il[0][:], nc.scalar.copy, "xt_w01")
         quant(g2q, g2s, gr2, 0, 256)
-        v2_il.append(turn("v2_3", vals2_sb[3], idx4, whole_s, 1))
-        scale_rows(3)
-        v2q = [quant_block("v2_%d" % b, v2_il[b]) for b in range(2)]
-        quant(g1q, g1s, gr1, 256, 512)
+        gather_s(w_pick[3][:], vals2_sb[3][:], idx4[:])
+        scale_rows(gr2, f2, 1)
+        quant_into(wq[:, 0:256], ws[:, 0:256], w_il[0][:])
+        gather_s(v_pick[0][:], vals_sb[0][:], idx[:])
+        turn(w_pick[2:4], 2, 5, w_il[1][:], nc.scalar.copy, "xt_w23")
+        scale_rows(gr1, f1, 0)
         quant(g2q, g2s, gr2, 256, 512)
-        v2q = v2q + [quant_block("v2_%d" % b, v2_il[b]) for b in range(2, 4)]
-
-        res = held([P, E // P, J], F32, "res")
-        for b in range(E // P):
-            last = b == E // P - 1
-            il = turn("v1_%d" % b, vals_sb[b], idx, gather_both if last else whole_s, b)
-            v1q = quant_block("v1_%d" % b, il)
-            pieces = [(0, 256, 6), (256, 512, 7)] if last else [(0, 512, b)]
-            accs = [bank([P, c1 - c0], bk, "acc") for c0, c1, bk in pieces]
-            for first, (vq, vs), gq, gs in ((True, v2q[b], g2q, g2s), (False, v1q, g1q, g1s)):
-                for acc, (c0, c1, bk) in zip(accs, pieces):
-                    nc.tensor.matmul_mx(
-                        out=acc[:],
-                        lhsT=vq[:].bitcast(FP8X4),
-                        lhsT_scale=vs[:],
-                        rhs=gq[:, c0:c1].bitcast(FP8X4),
-                        rhs_scale=gs[:, c0:c1],
-                        start=first,
-                        stop=not first,
-                    )
-            if last:
-                nc.vector.tensor_copy(out=res[:, b, 0:256], in_=accs[0][:])
-                nc.scalar.copy(out=res[:, b, 256:512], in_=accs[1][:])
-                nc.sync.dma_start(out[b * P : (b + 1) * P, 0:256], res[:, b, 0:256])
-                nc.scalar.dma_start(out[b * P : (b + 1) * P, 256:512], res[:, b, 256:512])
-            else:
-                nc.vector.tensor_copy(out=res[:, b, :], in_=accs[0][:])
-                nc.sync.dma_start(out[b * P : (b + 1) * P, :], res[:, b, :])
+        gather_s(v_pick[1][:], vals_sb[1][:], idx[:])
+        turn(v_pick[0:1], 1, 6, v_il0[:], nc.scalar.copy, "xt_v0")
+        accs = [bank([P, J], bk, "acc") for bk in range(4)]
+        for b in range(2):
+            product(accs[b], wq[:, blk(b)], ws[:, blk(b)], g2q, g2s, True)
+        scale_rows(gr1, f1, 1)
+        quant_into(wq[:, 256:512], ws[:, 256:512], w_il[1][:])
+        for b in range(2, 4):
+            product(accs[b], wq[:, blk(b)], ws[:, blk(b)], g2q, g2s, True)
+        gather_s(v_pick[2][:], vals_sb[2][:], idx[:])
+        turn(v_pick[1:2], 1, 7, v_il1[:], nc.scalar.copy, "xt_v1")
+        quant(g1q, g1s, gr1, 0, 512)
+        gather_both(v_pick[3][:], vals_sb[3][:], idx)
+        quant_into(vq[0][:, 0:P], vs[:, blk(0)], v_il0[:])
+        quant_into(vq[0][:, P : 2 * P], vs[:, blk(1)], v_il1[:])
+        turn(v_pick[2:3], 1, 4, v_il23[:, 0:P, :], nc.scalar.copy, "xt_v2")
+        turn(v_pick[3:4], 1, 5, v_il23[:, P : 2 * P, :], nc.vector.tensor_copy, "xt_v3")
+        for b in range(2):
+            product(accs[b], vq[0][:, blk(b)], vs[:, blk(b)], g1q, g1s, False)
+        quant_into(vq[1][:], vs[:, 256:512], v_il23[:])
+        for b in range(2, 4):
+            product(accs[b], vq[1][:, blk(b - 2)], vs[:, blk(b)], g1q, g1s, False)
+        for b in range(4):
+            copy = nc.vector.tensor_copy if b % 2 else nc.scalar.copy
+            copy(out=res[b][:], in_=accs[b][:])
+            nc.sync.dma_start(out[blk(b), :], res[b][:])

@@ -4,7 +4,7 @@ import concourse.mybir as mybir
 from concourse.masks import make_identity
 
 D, T, I, J, U, Z, E, Y = 512, 2048, 512, 512, 1024, 1024, 512, 1024
-FLOPS = 4 * 2 * 512 * 512 * 512
+FLOPS = 2 * (2 * D * I * J) + 2 * (2 * I * E * J)
 
 F32 = mybir.dt.float32
 BF16 = mybir.dt.bfloat16
@@ -19,8 +19,23 @@ MULT = mybir.AluOpType.mult
 
 P = 128
 PACK = 4
-CH = 128
-NCH = J // CH
+CHUNK = 128
+CHUNKS = J // CHUNK
+HALF = 256
+BLOCKS = E // P
+LAST = BLOCKS - 1
+KIB = 1024
+
+AT_USERS1 = 0
+AT_USERS3 = AT_USERS1 + 4 * Z
+AT_VALS2_LAST = AT_USERS3 + 4 * Z
+AT_VALS0 = AT_VALS2_LAST + 4 * Y
+AT_VALS2 = AT_VALS0 + 4 * T
+AT_VALS3 = AT_VALS2 + 4 * T
+
+BANK_TURN_VALS2 = (4, 5)
+BANK_TURN_VALS = (6, 7, 5, 6)
+BANK_LAST_HALVES = (3, 4)
 
 
 def tile_attend_tab_larger_twostores_kernel(
@@ -33,249 +48,268 @@ def tile_attend_tab_larger_twostores_kernel(
         reuse = ctx.enter_context(tc.tile_pool(name="reuse", bufs=1))
         psum = ctx.enter_context(tc.psum_pool(name="psum", bufs=1))
 
-        def held(shape, dtype, name):
-            return keep.tile(shape, dtype, name=name, align_bytes=64)
+        def sbuf(shape, dtype, name, at=None):
+            if at is None:
+                return keep.tile(shape, dtype, name=name, align_bytes=64)
+            return reuse.tile(shape, dtype, name=name, align_bytes=64, offset=at)
 
-        def placed(shape, dtype, name, kib):
-            return reuse.tile(shape, dtype, name=name, align_bytes=64, offset=kib * 1024)
+        def bank(shape, number, name):
+            return psum.tile(shape, F32, name=name, tag="bank%d" % number)
 
-        def bank(shape, b, name):
-            return psum.tile(shape, F32, name=name, tag="bank%d" % b)
+        def block(b):
+            return slice(b * P, (b + 1) * P)
+
+        def half(h):
+            return slice(h * HALF, (h + 1) * HALF)
 
         idx = lists.tile([P, I // 16], U16, name="idx")
         idx2 = lists.tile([P, J // 16], U16, name="idx2")
         idx3 = lists.tile([P, J // 16], U16, name="idx3")
         idx4 = lists.tile([P, I // 16], U16, name="idx4")
 
-        notes_sb = [held([P, U], F32, "notes%d" % t) for t in range(PACK)]
-        users_sb = [held([P, Z], F32, "users%d" % t) for t in range(PACK - 1)] + [placed([P, Z], F32, "users3", 0)]
-        vals_sb = [placed([P, T], F32, "vals%d" % b, 8 + 8 * b) for b in range(E // P)]
-        vals2_sb = [
-            placed([P, Y], F32, "valsb2", 4) if b == 2 else held([P, Y], F32, "valsb%d" % b) for b in range(E // P)
-        ]
-        kw_sb = held([P, T], U32, "kw_sb")
-        ks_sb = held([P, T], U8, "ks_sb")
-        f1 = held([P, PACK], F32, "f1")
-        f2 = held([P, PACK], F32, "f2")
-        ident = held([P, P], F32, "ident")
+        notes_in = [sbuf([P, U], F32, "notes_in%d" % t) for t in range(PACK)]
+        users_in = [sbuf([P, Z], F32, "users_in%d" % t, at) for t, at in enumerate((None, AT_USERS1, None, AT_USERS3))]
+        vals_in = [sbuf([P, T], F32, "vals_in%d" % b, at) for b, at in enumerate((AT_VALS0, None, AT_VALS2, AT_VALS3))]
+        vals2_in = [sbuf([P, Y], F32, "vals2_in%d" % b, at) for b, at in enumerate((None, None, None, AT_VALS2_LAST))]
+        key_words_in = sbuf([P, T], U32, "key_words_in")
+        key_scales_in = sbuf([P, T], U8, "key_scales_in")
+        f1 = sbuf([P, PACK], F32, "f1")
+        f2 = sbuf([P, PACK], F32, "f2")
+        ident = sbuf([P, P], F32, "ident")
 
-        nc.gpsimd.memset(ks_sb[:].bitcast(I32), 0)
+        nc.gpsimd.memset(key_scales_in[:].bitcast(I32), 0)
         nc.gpsimd.dma_start(out=f2[:], in_=rowf2.rearrange("(p r) o -> p (r o)", r=PACK))
         nc.gpsimd.dma_start(out=f1[:], in_=rowf.rearrange("(p r) o -> p (r o)", r=PACK))
         make_identity(nc, ident[:])
 
-        def load_scales(q):
+        def load_key_scales(q):
             nc.sync.dma_start(
-                out=ks_sb[32 * q : 32 * q + 4, :].bitcast(I32), in_=keys_scales[0, 4 * q : 4 * q + 4, :].bitcast(I32)
+                out=key_scales_in[32 * q : 32 * q + 4, :].bitcast(I32),
+                in_=keys_scales[0, 4 * q : 4 * q + 4, :].bitcast(I32),
             )
 
-        notes_pl = notes.rearrange("(p t) u -> t p u", t=PACK)
-        users_pl = users2.rearrange("(p t) u -> t p u", t=PACK)
-        nc.sync.dma_start(notes_sb[0][:], notes_pl[0])
+        notes_planes = notes.rearrange("(p t) u -> t p u", t=PACK)
+        users_planes = users2.rearrange("(p t) z -> t p z", t=PACK)
+        nc.sync.dma_start(notes_in[0][:], notes_planes[0])
         nc.sync.dma_start(idx2[:], offs2)
-        nc.sync.dma_start(notes_sb[1][:], notes_pl[1])
-        load_scales(0)
-        load_scales(1)
-        nc.sync.dma_start(notes_sb[2][:], notes_pl[2])
-        load_scales(2)
-        load_scales(3)
+        nc.sync.dma_start(notes_in[1][:], notes_planes[1])
+        load_key_scales(0)
+        load_key_scales(1)
+        nc.sync.dma_start(notes_in[2][:], notes_planes[2])
+        load_key_scales(2)
+        load_key_scales(3)
         nc.sync.dma_start(idx[:], offs)
-        nc.sync.dma_start(notes_sb[3][:], notes_pl[3])
-        nc.sync.dma_start(kw_sb[:].bitcast(I32), keys_words[0].rearrange("p n t -> p (n t)").bitcast(I32))
+        nc.sync.dma_start(notes_in[3][:], notes_planes[3])
+        nc.sync.dma_start(key_words_in[:].bitcast(I32), keys_words[0].rearrange("p n t -> p (n t)").bitcast(I32))
         nc.sync.dma_start(idx3[:], offs3)
-        nc.sync.dma_start(users_sb[0][:], users_pl[0])
-        nc.sync.dma_start(users_sb[1][:], users_pl[1])
+        nc.sync.dma_start(users_in[0][:], users_planes[0])
+        nc.sync.dma_start(users_in[1][:], users_planes[1])
         nc.sync.dma_start(idx4[:], offs4)
-        nc.sync.dma_start(users_sb[2][:], users_pl[2])
-        nc.sync.dma_start(users_sb[3][:], users_pl[3])
-        for b in range(E // P):
-            nc.sync.dma_start(vals2_sb[b][:], vals2[b * P : (b + 1) * P, :])
-        for b in range(E // P):
-            nc.sync.dma_start(vals_sb[b][:], vals[b * P : (b + 1) * P, :])
+        nc.sync.dma_start(users_in[2][:], users_planes[2])
+        nc.sync.dma_start(users_in[3][:], users_planes[3])
+        for b in range(BLOCKS):
+            nc.sync.dma_start(vals2_in[b][:], vals2[block(b), :])
+        for b in range(BLOCKS):
+            nc.sync.dma_start(vals_in[b][:], vals[block(b), :])
 
-        def gather_v(dst, window, offsets):
+        def gather_vector(dst, window, offsets):
             nc.vector.tensor_copy(dst, window.indirect(offsets))
 
-        def gather_s(dst, window, offsets):
+        def gather_scalar(dst, window, offsets):
             nc.scalar.activation(dst, window.indirect(offsets), COPY)
 
-        def gather_both(dst, window, offsets):
-            gather_v(dst[:, 0:256], window, offsets[:, 0:16])
-            gather_s(dst[:, 256:512], window, offsets[:, 16:32])
+        def gather_halves(dst, window, offsets):
+            gather_vector(dst[:, half(0)], window, offsets[:, 0 : HALF // 16])
+            gather_scalar(dst[:, half(1)], window, offsets[:, HALF // 16 : 2 * HALF // 16])
 
-        def weave(dst, planes, c0, c1, copy=nc.vector.tensor_copy):
+        def weave(woven, planes, h, copy):
             copy(
-                out=dst[:, c0:c1, :].rearrange("p (c i) t -> p c t i", i=4),
-                in_=planes[:, :, c0:c1].rearrange("p t (c i) -> p c t i", i=4),
+                out=woven[:, half(h), :].rearrange("p (c n) t -> p c t n", n=4),
+                in_=planes[:, :, half(h)].rearrange("p t (c n) -> p c t n", n=4),
             )
 
-        def quant(codes, scales, src, c0, c1):
-            nc.vector.quantize_mx(
-                out=codes[:, c0:c1].bitcast(FP8X4),
-                scales=scales[:, c0:c1],
-                in_=src[:, c0:c1, :].rearrange("p c t -> p (c t)"),
+        def quantise(words, scales, woven):
+            nc.vector.quantize_mx(out=words.bitcast(FP8X4), scales=scales, in_=woven.rearrange("p c t -> p (c t)"))
+
+        def multiply(acc, lhs_words, lhs_scales, rhs_words, rhs_scales, start, stop):
+            nc.tensor.matmul_mx(
+                out=acc,
+                lhsT=lhs_words.bitcast(FP8X4),
+                lhsT_scale=lhs_scales,
+                rhs=rhs_words.bitcast(FP8X4),
+                rhs_scale=rhs_scales,
+                start=start,
+                stop=stop,
             )
 
-        kq = held([P, I], U32, "kq")
-        kqs = held([P, I], U8, "kqs")
-        n_pl = held([P, PACK, J], BF16, "n_pl")
-        n_il = held([P, J, PACK], BF16, "n_il")
-        nq = held([P, J], U32, "nq")
-        nqs = held([P, J], U8, "nqs")
-        u_pl = held([P, PACK, J], BF16, "u_pl")
-        u_il = held([P, J, PACK], BF16, "u_il")
-        uq = held([P, J], U32, "uq")
-        uqs = held([P, J], U8, "uqs")
+        key_words = sbuf([P, I], U32, "key_words")
+        key_scales = sbuf([P, I], U8, "key_scales")
+        notes_picked = sbuf([P, PACK, J], BF16, "notes_picked")
+        notes_woven = sbuf([P, J, PACK], BF16, "notes_woven")
+        notes_words = sbuf([P, J], U32, "notes_words")
+        notes_scales = sbuf([P, J], U8, "notes_scales")
+        users_picked = sbuf([P, PACK, J], BF16, "users_picked")
+        users_woven = sbuf([P, J, PACK], BF16, "users_woven")
+        users_words = sbuf([P, J], U32, "users_words")
+        users_scales = sbuf([P, J], U8, "users_scales")
 
-        gather_s(n_pl[:, 0, :], notes_sb[0][:], idx2[:])
-        gather_v(n_pl[:, 1, :], notes_sb[1][:], idx2[:])
-        gather_v(kqs[:].rearrange("p (r s) -> p s r", r=PACK), ks_sb[:], idx[:])
-        gather_s(n_pl[:, 2, :], notes_sb[2][:], idx2[:])
-        gather_both(n_pl[:, 3, :], notes_sb[3][:], idx2)
-        weave(n_il, n_pl, 0, 256)
-        weave(n_il, n_pl, 256, 512, nc.scalar.copy)
-        quant(nq, nqs, n_il, 0, 256)
-        quant(nq, nqs, n_il, 256, 512)
-        gather_v(kq[:].rearrange("p (r s) -> p s r", r=PACK), kw_sb[:], idx[:])
+        gather_scalar(notes_picked[:, 0, :], notes_in[0][:], idx2[:])
+        gather_vector(notes_picked[:, 1, :], notes_in[1][:], idx2[:])
+        gather_vector(key_scales[:].rearrange("p (r s) -> p s r", r=PACK), key_scales_in[:], idx[:])
+        gather_scalar(notes_picked[:, 2, :], notes_in[2][:], idx2[:])
+        gather_halves(notes_picked[:, 3, :], notes_in[3][:], idx2)
+        weave(notes_woven, notes_picked, 0, nc.vector.tensor_copy)
+        weave(notes_woven, notes_picked, 1, nc.scalar.copy)
+        for h in range(2):
+            quantise(notes_words[:, half(h)], notes_scales[:, half(h)], notes_woven[:, half(h), :])
+        gather_vector(key_words[:].rearrange("p (r s) -> p s r", r=PACK), key_words_in[:], idx[:])
 
-        def scores(dst, codes, scales, c):
-            cols = slice(c * CH, (c + 1) * CH)
+        def table_chunk(acc, words, scales, c):
+            cols = slice(c * CHUNK, (c + 1) * CHUNK)
             for r in range(PACK):
-                rows = slice(r * P, (r + 1) * P)
-                nc.tensor.matmul_mx(
-                    out=dst[:, r, :],
-                    lhsT=kq[:, rows].bitcast(FP8X4),
-                    lhsT_scale=kqs[:, rows],
-                    rhs=codes[:, cols].bitcast(FP8X4),
-                    rhs_scale=scales[:, cols],
-                    start=True,
-                    stop=True,
+                multiply(
+                    acc[:, r, :], key_words[:, block(r)], key_scales[:, block(r)], words[:, cols], scales[:, cols], True, True
                 )
 
-        g1_half = [held([P, 2, CH, PACK], F32, "g1_lo"), placed([P, 2, CH, PACK], F32, "g1_hi", 0)]
-        g1_sb = [g1_half[c // 2][:, c % 2] for c in range(NCH)]
-        gather_s(u_pl[:, 0, :], users_sb[0][:], idx3[:])
-        gather_v(u_pl[:, 1, :], users_sb[1][:], idx3[:])
-        g1 = [bank([P, PACK, CH], c, "g1") for c in range(NCH)]
-        for c in range(NCH):
-            scores(g1[c], nq, nqs, c)
-        for c in range(2):
-            nc.scalar.copy(out=g1_sb[c], in_=g1[c][:].rearrange("p r j -> p j r"))
-        gather_v(u_pl[:, 2, :], users_sb[2][:], idx3[:])
-        gather_both(u_pl[:, 3, :], users_sb[3][:], idx3)
-        for c in range(2, NCH):
-            nc.scalar.copy(out=g1_sb[c], in_=g1[c][:].rearrange("p r j -> p j r"))
+        g1_pairs = [sbuf([P, 2, CHUNK, PACK], F32, "g1_pair%d" % n, at) for n, at in enumerate((AT_USERS1, AT_USERS3))]
+        g1 = [g1_pairs[c // 2][:, c % 2] for c in range(CHUNKS)]
+        gather_scalar(users_picked[:, 0, :], users_in[0][:], idx3[:])
+        gather_scalar(users_picked[:, 1, :], users_in[1][:], idx3[:])
+        g1_banks = [bank([P, PACK, CHUNK], c, "g1_bank") for c in range(CHUNKS)]
+        for c in range(CHUNKS):
+            table_chunk(g1_banks[c], notes_words, notes_scales, c)
+        for c in (0, 1):
+            nc.scalar.copy(out=g1[c], in_=g1_banks[c][:].rearrange("p r j -> p j r"))
+        gather_vector(users_picked[:, 2, :], users_in[2][:], idx3[:])
+        gather_halves(users_picked[:, 3, :], users_in[3][:], idx3)
+        for c in (2, 3):
+            nc.scalar.copy(out=g1[c], in_=g1_banks[c][:].rearrange("p r j -> p j r"))
 
-        g0 = held([P, J, PACK], F32, "g0")
-        gr1 = held([P, J, PACK], BF16, "gr1")
-        gr2 = held([P, J, PACK], BF16, "gr2")
-        g1q = held([P, J], U32, "g1q")
-        g1s = held([P, J], U8, "g1s")
-        g2q = held([P, J], U32, "g2q")
-        g2s = held([P, J], U8, "g2s")
+        g0 = sbuf([P, J, PACK], F32, "g0")
+        gr1 = sbuf([P, J, PACK], BF16, "gr1")
+        gr2 = sbuf([P, J, PACK], BF16, "gr2")
+        gr1_words = sbuf([P, J], U32, "gr1_words")
+        gr1_scales = sbuf([P, J], U8, "gr1_scales")
+        gr2_words = sbuf([P, J], U32, "gr2_words")
+        gr2_scales = sbuf([P, J], U8, "gr2_scales")
 
-        weave(u_il, u_pl, 0, 256)
-        weave(u_il, u_pl, 256, 512)
-        quant(uq, uqs, u_il, 0, 256)
-        quant(uq, uqs, u_il, 256, 512)
+        for h in range(2):
+            weave(users_woven, users_picked, h, nc.vector.tensor_copy)
+            quantise(users_words[:, half(h)], users_scales[:, half(h)], users_woven[:, half(h), :])
 
         def larger(c):
-            cols = slice(c * CH, (c + 1) * CH)
-            g2 = bank([P, PACK, CH], c, "g2")
-            scores(g2, uq, uqs, c)
+            g2_bank = bank([P, PACK, CHUNK], c, "g2_bank")
+            table_chunk(g2_bank, users_words, users_scales, c)
             nc.vector.tensor_tensor(
-                out=g0[:, cols, :], in0=g2[:].rearrange("p r j -> p j r"), in1=g1_sb[c], op=MAX
+                out=g0[:, c * CHUNK : (c + 1) * CHUNK, :], in0=g2_bank[:].rearrange("p r j -> p j r"), in1=g1[c], op=MAX
             )
 
-        def scale_rows(dst, f, h):
-            cols = slice(h * 256, (h + 1) * 256)
+        def scale_rows(gr, f, h):
             nc.vector.tensor_tensor(
-                out=dst[:, cols, :],
-                in0=g0[:, cols, :],
-                in1=f[:].unsqueeze(1).to_broadcast([P, 256, PACK]),
+                out=gr[:, half(h), :],
+                in0=g0[:, half(h), :],
+                in1=f[:].unsqueeze(1).to_broadcast([P, HALF, PACK]),
                 op=MULT,
             )
 
-        def turn(picked, nblk, bk, il, copy, name):
-            xt = bank([P, nblk, 2, P], bk, name)
-            for n in range(nblk):
-                words = picked[n][:].bitcast(F32)
+        def turn(picked, number, woven, copy):
+            count = len(picked)
+            turned = bank([P, count, 2, P], number, "turned")
+            for n in range(count):
+                pairs = picked[n][:].bitcast(F32)
                 for u in range(2):
-                    nc.tensor.transpose(xt[:, n, u, :], words[:, u : I // 2 : 2], ident[:])
+                    nc.tensor.transpose(turned[:, n, u, :], pairs[:, u : I // 2 : 2], ident[:])
             copy(
-                out=il.rearrange("p e t -> p (e t)").bitcast(F32).rearrange("p (n e u) -> p n e u", n=nblk, u=2),
-                in_=xt[:].rearrange("p n u e -> p n e u"),
+                out=woven.rearrange("p e t -> p (e t)").bitcast(F32).rearrange("p (n e u) -> p n e u", n=count, u=2),
+                in_=turned[:].rearrange("p n u e -> p n e u"),
             )
 
-        w_pick = [held([P, I], BF16, "w_pick%d" % b) for b in range(4)]
-        v_pick = [held([P, I], BF16, "v_pick%d" % b) for b in range(4)]
-        w_il = [placed([P, 256, PACK], BF16, "w_il01", 4), placed([P, 256, PACK], BF16, "w_il23", 8)]
-        v_il0 = placed([P, P, PACK], BF16, "v_il0", 16)
-        v_il1 = placed([P, P, PACK], BF16, "v_il1", 24)
-        v_il23 = placed([P, 256, PACK], BF16, "v_il23", 36)
-        wq = held([P, E], U32, "wq")
-        ws = held([P, E], U8, "ws")
-        vq = [placed([P, 256], U32, "vq01", 38), held([P, 256], U32, "vq23")]
-        vs = held([P, E], U8, "vs")
-        res = [placed([P, J], F32, "res0", 32), placed([P, J], F32, "res1", 34), held([P, J], F32, "res2"), held([P, J], F32, "res3")]
+        vt2_picked = [sbuf([P, I], BF16, "vt2_picked%d" % b) for b in range(BLOCKS)]
+        vt1_picked = [sbuf([P, I], BF16, "vt1_picked%d" % b) for b in range(BLOCKS)]
+        vt2_woven = [sbuf([P, HALF, PACK], BF16, "vt2_woven%d" % h, at) for h, at in enumerate((AT_VALS2_LAST, AT_VALS0))]
+        vt1_woven = [
+            sbuf([P, P, PACK], BF16, "vt1_woven%d" % b, at)
+            for b, at in enumerate((AT_VALS2, AT_VALS2 + 4 * KIB, AT_VALS3, None))
+        ]
+        vt2_words = [sbuf([P, HALF], U32, "vt2_words%d" % h) for h in range(2)]
+        vt1_words = [sbuf([P, P], U32, "vt1_words%d" % b, at) for b, at in enumerate((None, AT_VALS3 + 6 * KIB, None, None))]
+        rows = [sbuf([P, J], F32, "rows%d" % b, at) for b, at in enumerate((AT_VALS3 + 2 * KIB, None, None, None))]
+        vt2_scales = sbuf([P, E], U8, "vt2_scales")
+        vt1_scales = sbuf([P, E], U8, "vt1_scales")
 
-        def quant_into(codes, scales, src):
-            nc.vector.quantize_mx(out=codes.bitcast(FP8X4), scales=scales, in_=src.rearrange("p c t -> p (c t)"))
+        def pick_vt2(b):
+            gather_scalar(vt2_picked[b][:], vals2_in[b][:], idx4[:])
 
-        def product(acc, lq, ls, gq, gs, first):
-            nc.tensor.matmul_mx(
-                out=acc[:],
-                lhsT=lq.bitcast(FP8X4),
-                lhsT_scale=ls,
-                rhs=gq[:].bitcast(FP8X4),
-                rhs_scale=gs[:],
-                start=first,
-                stop=not first,
-            )
+        def pick_vt1(b):
+            gather_scalar(vt1_picked[b][:], vals_in[b][:], idx[:])
 
-        def blk(b):
-            return slice(b * P, (b + 1) * P)
+        def turn_vt2(h):
+            turn(vt2_picked[2 * h : 2 * h + 2], BANK_TURN_VALS2[h], vt2_woven[h][:], nc.scalar.copy)
 
-        gather_s(w_pick[0][:], vals2_sb[0][:], idx4[:])
-        larger(0)
-        larger(1)
-        gather_s(w_pick[1][:], vals2_sb[1][:], idx4[:])
-        larger(2)
+        def turn_vt1(b, copy):
+            turn(vt1_picked[b : b + 1], BANK_TURN_VALS[b], vt1_woven[b][:], copy)
+
+        def open_sum(acc, b, cols):
+            words = vt2_words[b // 2][:, block(b % 2)]
+            multiply(acc, words, vt2_scales[:, block(b)], gr2_words[:, cols], gr2_scales[:, cols], True, False)
+
+        def close_sum(acc, b, cols):
+            multiply(acc, vt1_words[b][:], vt1_scales[:, block(b)], gr1_words[:, cols], gr1_scales[:, cols], False, True)
+
+        def quantise_vt1(b):
+            quantise(vt1_words[b][:], vt1_scales[:, block(b)], vt1_woven[b][:])
+
+        def store_block(b):
+            nc.scalar.copy(out=rows[b][:], in_=sums[b][:])
+            nc.sync.dma_start(out[block(b), :], rows[b][:])
+
+        whole = slice(0, J)
+        pick_vt2(0)
+        pick_vt2(1)
+        for c in range(CHUNKS):
+            larger(c)
         scale_rows(gr2, f2, 0)
-        larger(3)
-        gather_s(w_pick[2][:], vals2_sb[2][:], idx4[:])
-        turn(w_pick[0:2], 2, 4, w_il[0][:], nc.scalar.copy, "xt_w01")
-        quant(g2q, g2s, gr2, 0, 256)
-        gather_s(w_pick[3][:], vals2_sb[3][:], idx4[:])
+        pick_vt2(2)
+        pick_vt2(3)
+        turn_vt2(0)
         scale_rows(gr2, f2, 1)
-        quant_into(wq[:, 0:256], ws[:, 0:256], w_il[0][:])
-        gather_s(v_pick[0][:], vals_sb[0][:], idx[:])
-        turn(w_pick[2:4], 2, 5, w_il[1][:], nc.scalar.copy, "xt_w23")
+        quantise(vt2_words[0][:], vt2_scales[:, half(0)], vt2_woven[0][:])
+        pick_vt1(0)
+        turn_vt2(1)
+        quantise(gr2_words[:], gr2_scales[:], gr2[:])
         scale_rows(gr1, f1, 0)
-        quant(g2q, g2s, gr2, 256, 512)
-        gather_s(v_pick[1][:], vals_sb[1][:], idx[:])
-        turn(v_pick[0:1], 1, 6, v_il0[:], nc.scalar.copy, "xt_v0")
-        accs = [bank([P, J], bk, "acc") for bk in range(4)]
-        for b in range(2):
-            product(accs[b], wq[:, blk(b)], ws[:, blk(b)], g2q, g2s, True)
+        pick_vt1(1)
+
+        sums = [bank([P, J], b, "sum") for b in range(LAST)]
+        last_halves = [bank([P, HALF], number, "last_half") for number in BANK_LAST_HALVES]
+        for b in (0, 1):
+            open_sum(sums[b][:], b, whole)
         scale_rows(gr1, f1, 1)
-        quant_into(wq[:, 256:512], ws[:, 256:512], w_il[1][:])
-        for b in range(2, 4):
-            product(accs[b], wq[:, blk(b)], ws[:, blk(b)], g2q, g2s, True)
-        gather_s(v_pick[2][:], vals_sb[2][:], idx[:])
-        turn(v_pick[1:2], 1, 7, v_il1[:], nc.scalar.copy, "xt_v1")
-        quant(g1q, g1s, gr1, 0, 512)
-        gather_both(v_pick[3][:], vals_sb[3][:], idx)
-        quant_into(vq[0][:, 0:P], vs[:, blk(0)], v_il0[:])
-        quant_into(vq[0][:, P : 2 * P], vs[:, blk(1)], v_il1[:])
-        turn(v_pick[2:3], 1, 4, v_il23[:, 0:P, :], nc.scalar.copy, "xt_v2")
-        turn(v_pick[3:4], 1, 5, v_il23[:, P : 2 * P, :], nc.vector.tensor_copy, "xt_v3")
-        for b in range(2):
-            product(accs[b], vq[0][:, blk(b)], vs[:, blk(b)], g1q, g1s, False)
-        quant_into(vq[1][:], vs[:, 256:512], v_il23[:])
-        for b in range(2, 4):
-            product(accs[b], vq[1][:, blk(b - 2)], vs[:, blk(b)], g1q, g1s, False)
-        for b in range(4):
-            copy = nc.vector.tensor_copy if b % 2 else nc.scalar.copy
-            copy(out=res[b][:], in_=accs[b][:])
-            nc.sync.dma_start(out[blk(b), :], res[b][:])
+        quantise(vt2_words[1][:], vt2_scales[:, half(1)], vt2_woven[1][:])
+        open_sum(sums[2][:], 2, whole)
+        for h in range(2):
+            open_sum(last_halves[h][:], LAST, half(h))
+        pick_vt1(2)
+        for b in (0, 1):
+            turn_vt1(b, nc.scalar.copy)
+        quantise(gr1_words[:], gr1_scales[:], gr1[:])
+
+        quantise_vt1(0)
+        close_sum(sums[0][:], 0, whole)
+        gather_halves(vt1_picked[LAST][:], vals_in[LAST][:], idx)
+        turn_vt1(2, nc.scalar.copy)
+        quantise_vt1(1)
+        close_sum(sums[1][:], 1, whole)
+        turn_vt1(LAST, nc.vector.tensor_copy)
+        store_block(0)
+        quantise_vt1(2)
+        close_sum(sums[2][:], 2, whole)
+        store_block(1)
+        store_block(2)
+        quantise_vt1(LAST)
+        for h in range(2):
+            close_sum(last_halves[h][:], LAST, half(h))
+        nc.vector.tensor_copy(out=rows[LAST][:, half(0)], in_=last_halves[0][:])
+        nc.scalar.copy(out=rows[LAST][:, half(1)], in_=last_halves[1][:])
+        nc.sync.dma_start(out[block(LAST), half(0)], rows[LAST][:, half(0)])
+        nc.scalar.dma_start(out[block(LAST), half(1)], rows[LAST][:, half(1)])

from contextlib import ExitStack

import concourse.mybir as mybir
from concourse.masks import make_identity

D, T, I, J, U, Z, E, Y = 512, 2048, 512, 512, 1024, 1024, 512, 1024
FLOPS = 2 * (2 * D * I * J) + 2 * (2 * I * E * J)

F32 = mybir.dt.float32
BF16 = mybir.dt.bfloat16
I32 = mybir.dt.int32
U32 = mybir.dt.uint32
U16 = mybir.dt.uint16
U8 = mybir.dt.uint8
FP8X4 = mybir.dt.float8_e4m3fn_x4
COPY = mybir.ActivationFunctionType.Copy
MAX = mybir.AluOpType.max
MULT = mybir.AluOpType.mult

P = 128
PACK = 4
CHUNK = 128
CHUNKS = J // CHUNK
HALF = 256
BLOCKS = E // P
LAST = BLOCKS - 1
KIB = 1024

AT_USERS1 = 0
AT_USERS3 = AT_USERS1 + 4 * Z
AT_VALS2_LAST = AT_USERS3 + 4 * Z
AT_VALS0 = AT_VALS2_LAST + 4 * Y
AT_VALS2 = AT_VALS0 + 4 * T
AT_VALS3 = AT_VALS2 + 4 * T

BANK_TURN_VALS2 = (4, 5)
BANK_TURN_VALS = (6, 7, 5, 6)
BANK_LAST_HALVES = (3, 4)


def tile_attend_tab_larger_twostores_kernel(
    tc, keys_words, keys_scales, notes, users2, rowf, rowf2, vals, vals2, offs, offs2, offs3, offs4, out
):
    nc = tc.nc
    with ExitStack() as ctx:
        lists = ctx.enter_context(tc.tile_pool(name="lists", bufs=1))
        keep = ctx.enter_context(tc.tile_pool(name="keep", bufs=1))
        reuse = ctx.enter_context(tc.tile_pool(name="reuse", bufs=1))
        psum = ctx.enter_context(tc.psum_pool(name="psum", bufs=1))

        def sbuf(shape, dtype, name, at=None):
            if at is None:
                return keep.tile(shape, dtype, name=name, align_bytes=64)
            return reuse.tile(shape, dtype, name=name, align_bytes=64, offset=at)

        def bank(shape, number, name):
            return psum.tile(shape, F32, name=name, tag="bank%d" % number)

        def block(b):
            return slice(b * P, (b + 1) * P)

        def half(h):
            return slice(h * HALF, (h + 1) * HALF)

        idx = lists.tile([P, I // 16], U16, name="idx")
        idx2 = lists.tile([P, J // 16], U16, name="idx2")
        idx3 = lists.tile([P, J // 16], U16, name="idx3")
        idx4 = lists.tile([P, I // 16], U16, name="idx4")

        notes_in = [sbuf([P, U], F32, "notes_in%d" % t) for t in range(PACK)]
        users_in = [sbuf([P, Z], F32, "users_in%d" % t, at) for t, at in enumerate((None, AT_USERS1, None, AT_USERS3))]
        vals_in = [sbuf([P, T], F32, "vals_in%d" % b, at) for b, at in enumerate((AT_VALS0, None, AT_VALS2, AT_VALS3))]
        vals2_in = [sbuf([P, Y], F32, "vals2_in%d" % b, at) for b, at in enumerate((None, None, None, AT_VALS2_LAST))]
        key_words_in = sbuf([P, T], U32, "key_words_in")
        key_scales_in = sbuf([P, T], U8, "key_scales_in")
        f1 = sbuf([P, PACK], F32, "f1")
        f2 = sbuf([P, PACK], F32, "f2")
        ident = sbuf([P, P], F32, "ident")

        nc.gpsimd.memset(key_scales_in[:].bitcast(I32), 0)
        nc.gpsimd.dma_start(out=f2[:], in_=rowf2.rearrange("(p r) o -> p (r o)", r=PACK))
        nc.gpsimd.dma_start(out=f1[:], in_=rowf.rearrange("(p r) o -> p (r o)", r=PACK))
        make_identity(nc, ident[:])

        def load_key_scales(q):
            nc.sync.dma_start(
                out=key_scales_in[32 * q : 32 * q + 4, :].bitcast(I32),
                in_=keys_scales[0, 4 * q : 4 * q + 4, :].bitcast(I32),
            )

        notes_planes = notes.rearrange("(p t) u -> t p u", t=PACK)
        users_planes = users2.rearrange("(p t) z -> t p z", t=PACK)
        nc.sync.dma_start(notes_in[0][:], notes_planes[0])
        nc.sync.dma_start(idx2[:], offs2)
        nc.sync.dma_start(notes_in[1][:], notes_planes[1])
        load_key_scales(0)
        load_key_scales(1)
        nc.sync.dma_start(notes_in[2][:], notes_planes[2])
        load_key_scales(2)
        load_key_scales(3)
        nc.sync.dma_start(idx[:], offs)
        nc.sync.dma_start(notes_in[3][:], notes_planes[3])
        nc.sync.dma_start(key_words_in[:].bitcast(I32), keys_words[0].rearrange("p n t -> p (n t)").bitcast(I32))
        nc.sync.dma_start(idx3[:], offs3)
        nc.sync.dma_start(users_in[0][:], users_planes[0])
        nc.sync.dma_start(users_in[1][:], users_planes[1])
        nc.sync.dma_start(idx4[:], offs4)
        nc.sync.dma_start(users_in[2][:], users_planes[2])
        nc.sync.dma_start(users_in[3][:], users_planes[3])
        for b in range(BLOCKS):
            nc.sync.dma_start(vals2_in[b][:], vals2[block(b), :])
        for b in range(BLOCKS):
            nc.sync.dma_start(vals_in[b][:], vals[block(b), :])

        def gather_vector(dst, window, offsets):
            nc.vector.tensor_copy(dst, window.indirect(offsets))

        def gather_scalar(dst, window, offsets):
            nc.scalar.activation(dst, window.indirect(offsets), COPY)

        def gather_halves(dst, window, offsets):
            gather_vector(dst[:, half(0)], window, offsets[:, 0 : HALF // 16])
            gather_scalar(dst[:, half(1)], window, offsets[:, HALF // 16 : 2 * HALF // 16])

        def weave(woven, planes, h, copy):
            copy(
                out=woven[:, half(h), :].rearrange("p (c n) t -> p c t n", n=4),
                in_=planes[:, :, half(h)].rearrange("p t (c n) -> p c t n", n=4),
            )

        def quantise(words, scales, woven):
            nc.vector.quantize_mx(out=words.bitcast(FP8X4), scales=scales, in_=woven.rearrange("p c t -> p (c t)"))

        def multiply(acc, lhs_words, lhs_scales, rhs_words, rhs_scales, start, stop):
            nc.tensor.matmul_mx(
                out=acc,
                lhsT=lhs_words.bitcast(FP8X4),
                lhsT_scale=lhs_scales,
                rhs=rhs_words.bitcast(FP8X4),
                rhs_scale=rhs_scales,
                start=start,
                stop=stop,
            )

        key_words = sbuf([P, I], U32, "key_words")
        key_scales = sbuf([P, I], U8, "key_scales")
        notes_picked = sbuf([P, PACK, J], BF16, "notes_picked")
        notes_woven = sbuf([P, J, PACK], BF16, "notes_woven")
        notes_words = sbuf([P, J], U32, "notes_words")
        notes_scales = sbuf([P, J], U8, "notes_scales")
        users_picked = sbuf([P, PACK, J], BF16, "users_picked")
        users_woven = sbuf([P, J, PACK], BF16, "users_woven")
        users_words = sbuf([P, J], U32, "users_words")
        users_scales = sbuf([P, J], U8, "users_scales")

        gather_scalar(notes_picked[:, 0, :], notes_in[0][:], idx2[:])
        gather_vector(notes_picked[:, 1, :], notes_in[1][:], idx2[:])
        gather_vector(key_scales[:].rearrange("p (r s) -> p s r", r=PACK), key_scales_in[:], idx[:])
        gather_scalar(notes_picked[:, 2, :], notes_in[2][:], idx2[:])
        gather_halves(notes_picked[:, 3, :], notes_in[3][:], idx2)
        weave(notes_woven, notes_picked, 0, nc.vector.tensor_copy)
        weave(notes_woven, notes_picked, 1, nc.scalar.copy)
        for h in range(2):
            quantise(notes_words[:, half(h)], notes_scales[:, half(h)], notes_woven[:, half(h), :])
        gather_vector(key_words[:].rearrange("p (r s) -> p s r", r=PACK), key_words_in[:], idx[:])

        def table_chunk(acc, words, scales, c):
            cols = slice(c * CHUNK, (c + 1) * CHUNK)
            for r in range(PACK):
                multiply(
                    acc[:, r, :], key_words[:, block(r)], key_scales[:, block(r)], words[:, cols], scales[:, cols], True, True
                )

        g1_pairs = [sbuf([P, 2, CHUNK, PACK], F32, "g1_pair%d" % n, at) for n, at in enumerate((AT_USERS1, AT_USERS3))]
        g1 = [g1_pairs[c // 2][:, c % 2] for c in range(CHUNKS)]
        gather_scalar(users_picked[:, 0, :], users_in[0][:], idx3[:])
        gather_scalar(users_picked[:, 1, :], users_in[1][:], idx3[:])
        g1_banks = [bank([P, PACK, CHUNK], c, "g1_bank") for c in range(CHUNKS)]
        for c in range(CHUNKS):
            table_chunk(g1_banks[c], notes_words, notes_scales, c)
        for c in (0, 1):
            nc.scalar.copy(out=g1[c], in_=g1_banks[c][:].rearrange("p r j -> p j r"))
        gather_vector(users_picked[:, 2, :], users_in[2][:], idx3[:])
        gather_halves(users_picked[:, 3, :], users_in[3][:], idx3)
        for c in (2, 3):
            nc.scalar.copy(out=g1[c], in_=g1_banks[c][:].rearrange("p r j -> p j r"))

        g0 = sbuf([P, J, PACK], F32, "g0")
        gr1 = sbuf([P, J, PACK], BF16, "gr1")
        gr2 = sbuf([P, J, PACK], BF16, "gr2")
        gr1_words = sbuf([P, J], U32, "gr1_words")
        gr1_scales = sbuf([P, J], U8, "gr1_scales")
        gr2_words = sbuf([P, J], U32, "gr2_words")
        gr2_scales = sbuf([P, J], U8, "gr2_scales")

        for h in range(2):
            weave(users_woven, users_picked, h, nc.vector.tensor_copy)
            quantise(users_words[:, half(h)], users_scales[:, half(h)], users_woven[:, half(h), :])

        def larger(c):
            g2_bank = bank([P, PACK, CHUNK], c, "g2_bank")
            table_chunk(g2_bank, users_words, users_scales, c)
            nc.vector.tensor_tensor(
                out=g0[:, c * CHUNK : (c + 1) * CHUNK, :], in0=g2_bank[:].rearrange("p r j -> p j r"), in1=g1[c], op=MAX
            )

        def scale_rows(gr, f, h):
            nc.vector.tensor_tensor(
                out=gr[:, half(h), :],
                in0=g0[:, half(h), :],
                in1=f[:].unsqueeze(1).to_broadcast([P, HALF, PACK]),
                op=MULT,
            )

        def turn(picked, number, woven, copy):
            count = len(picked)
            turned = bank([P, count, 2, P], number, "turned")
            for n in range(count):
                pairs = picked[n][:].bitcast(F32)
                for u in range(2):
                    nc.tensor.transpose(turned[:, n, u, :], pairs[:, u : I // 2 : 2], ident[:])
            copy(
                out=woven.rearrange("p e t -> p (e t)").bitcast(F32).rearrange("p (n e u) -> p n e u", n=count, u=2),
                in_=turned[:].rearrange("p n u e -> p n e u"),
            )

        vt2_picked = [sbuf([P, I], BF16, "vt2_picked%d" % b) for b in range(BLOCKS)]
        vt1_picked = [sbuf([P, I], BF16, "vt1_picked%d" % b) for b in range(BLOCKS)]
        vt2_woven = [sbuf([P, HALF, PACK], BF16, "vt2_woven%d" % h, at) for h, at in enumerate((AT_VALS2_LAST, AT_VALS0))]
        vt1_woven = [
            sbuf([P, P, PACK], BF16, "vt1_woven%d" % b, at)
            for b, at in enumerate((AT_VALS2, AT_VALS2 + 4 * KIB, AT_VALS3, None))
        ]
        vt2_words = [sbuf([P, HALF], U32, "vt2_words%d" % h) for h in range(2)]
        vt1_words = [sbuf([P, P], U32, "vt1_words%d" % b, at) for b, at in enumerate((None, AT_VALS3 + 6 * KIB, None, None))]
        rows = [sbuf([P, J], F32, "rows%d" % b, at) for b, at in enumerate((AT_VALS3 + 2 * KIB, None, None, None))]
        vt2_scales = sbuf([P, E], U8, "vt2_scales")
        vt1_scales = sbuf([P, E], U8, "vt1_scales")

        def pick_vt2(b):
            gather_scalar(vt2_picked[b][:], vals2_in[b][:], idx4[:])

        def pick_vt1(b):
            gather_scalar(vt1_picked[b][:], vals_in[b][:], idx[:])

        def turn_vt2(h):
            turn(vt2_picked[2 * h : 2 * h + 2], BANK_TURN_VALS2[h], vt2_woven[h][:], nc.scalar.copy)

        def turn_vt1(b, copy):
            turn(vt1_picked[b : b + 1], BANK_TURN_VALS[b], vt1_woven[b][:], copy)

        def open_sum(acc, b, cols):
            words = vt2_words[b // 2][:, block(b % 2)]
            multiply(acc, words, vt2_scales[:, block(b)], gr2_words[:, cols], gr2_scales[:, cols], True, False)

        def close_sum(acc, b, cols):
            multiply(acc, vt1_words[b][:], vt1_scales[:, block(b)], gr1_words[:, cols], gr1_scales[:, cols], False, True)

        def quantise_vt1(b):
            quantise(vt1_words[b][:], vt1_scales[:, block(b)], vt1_woven[b][:])

        def store_block(b):
            nc.scalar.copy(out=rows[b][:], in_=sums[b][:])
            nc.sync.dma_start(out[block(b), :], rows[b][:])

        whole = slice(0, J)
        pick_vt2(0)
        pick_vt2(1)
        for c in range(CHUNKS):
            larger(c)
        scale_rows(gr2, f2, 0)
        pick_vt2(2)
        pick_vt2(3)
        turn_vt2(0)
        scale_rows(gr2, f2, 1)
        quantise(vt2_words[0][:], vt2_scales[:, half(0)], vt2_woven[0][:])
        pick_vt1(0)
        turn_vt2(1)
        quantise(gr2_words[:], gr2_scales[:], gr2[:])
        scale_rows(gr1, f1, 0)
        pick_vt1(1)

        sums = [bank([P, J], b, "sum") for b in range(LAST)]
        last_halves = [bank([P, HALF], number, "last_half") for number in BANK_LAST_HALVES]
        for b in (0, 1):
            open_sum(sums[b][:], b, whole)
        scale_rows(gr1, f1, 1)
        quantise(vt2_words[1][:], vt2_scales[:, half(1)], vt2_woven[1][:])
        open_sum(sums[2][:], 2, whole)
        for h in range(2):
            open_sum(last_halves[h][:], LAST, half(h))
        pick_vt1(2)
        for b in (0, 1):
            turn_vt1(b, nc.scalar.copy)
        quantise(gr1_words[:], gr1_scales[:], gr1[:])

        quantise_vt1(0)
        close_sum(sums[0][:], 0, whole)
        gather_halves(vt1_picked[LAST][:], vals_in[LAST][:], idx)
        turn_vt1(2, nc.scalar.copy)
        quantise_vt1(1)
        close_sum(sums[1][:], 1, whole)
        turn_vt1(LAST, nc.vector.tensor_copy)
        store_block(0)
        quantise_vt1(2)
        close_sum(sums[2][:], 2, whole)
        store_block(1)
        store_block(2)
        quantise_vt1(LAST)
        for h in range(2):
            close_sum(last_halves[h][:], LAST, half(h))
        nc.vector.tensor_copy(out=rows[LAST][:, half(0)], in_=last_halves[0][:])
        nc.scalar.copy(out=rows[LAST][:, half(1)], in_=last_halves[1][:])
        nc.sync.dma_start(out[block(LAST), half(0)], rows[LAST][:, half(0)])
        nc.scalar.dma_start(out[block(LAST), half(1)], rows[LAST][:, half(1)])
